import numpy as np
import ml_dtypes


def mxq(x, axis, fmt="e4m3"):
    dtype, down = {"e4m3": (ml_dtypes.float8_e4m3fn, 7), "e5m2": (ml_dtypes.float8_e5m2, 14)}[fmt]
    v = np.moveaxis(np.asarray(x, np.float32).astype(ml_dtypes.bfloat16).astype(np.float64), axis, -1)
    blocks = v.reshape(v.shape[:-1] + (-1, 32))
    amax = np.abs(blocks).max(-1, keepdims=True)
    byte = np.maximum(np.where(amax > 0, np.frexp(amax)[1] - 1 + 127, 0) - down, 1)
    scale = np.exp2(byte - 127.0)
    codes = (blocks / scale).astype(np.float32).astype(dtype).astype(np.float64)
    return np.moveaxis((codes * scale).reshape(v.shape), -1, axis)


WIDE = False


def mx_kscale(k):
    if not WIDE:
        return np.ones(k)
    levels = np.array([30, -30])
    if k % 512:
        return np.exp2(np.random.permutation(np.resize(levels, k // 32))).repeat(32)
    a = np.empty((k // 512, 16))
    for p in range(k // 512):
        a[p, :8] = np.random.permutation(np.resize(levels, 8))
        for g in range(8):
            far = levels[np.abs(levels - a[p, g]) >= 10]
            a[p, g + 8] = far[np.random.randint(len(far))]
    return np.exp2(a.ravel()).repeat(32)


def f64(x):
    return np.asarray(x).astype(np.float64)


def striped(idx):
    return np.tile(np.asarray(idx).reshape(-1, 16).T, (8, 1)).astype(np.uint16)


def unstriped(offs):
    return offs[:16].T.reshape(-1).astype(np.int64)


E2M1 = np.array([0.0, 0.5, 1.0, 1.5, 2.0, 3.0, 4.0, 6.0, -0.0, -0.5, -1.0, -1.5, -2.0, -3.0, -4.0, -6.0])


def pack_weight(w, fmt):
    k, n = w.shape
    w = f64(np.asarray(w, np.float32).astype(ml_dtypes.bfloat16)).reshape(k // 32, 32, n)
    amax = np.abs(w).max(1)
    if fmt in ("e4m3", "e5m2"):
        byte = np.frexp(amax)[1] - 1 + 127 - (7 if fmt == "e4m3" else 14)
    else:
        mant, ex = np.frexp(amax / 6.0)
        byte = np.where(mant > 0.5, ex, ex - 1) + 127
    byte = np.clip(np.where(amax > 0, byte, 1), 1, 254)
    scaled = (w * np.exp2(127.0 - byte)[:, None, :]).reshape(k, n).astype(np.float32)
    by_word = np.ascontiguousarray(scaled.reshape(k // 512, 128, 4, n).transpose(0, 1, 3, 2))
    if fmt in ("e4m3", "e5m2"):
        words = by_word.astype(ml_dtypes.float8_e4m3fn if fmt == "e4m3" else ml_dtypes.float8_e5m2).view(np.uint8)
    else:
        c = by_word.astype(ml_dtypes.float4_e2m1fn).view(np.uint8) & 0xF
        words = (c[..., 0::2] | (c[..., 1::2] << 4)).reshape(k // 512, 128, 2 * n)
    return np.ascontiguousarray(words), np.ascontiguousarray(byte.astype(np.uint8).reshape(k // 512, 16, n))


def unpack_weight(words, scales, fmt):
    g, _, n = scales.shape
    words = np.ascontiguousarray(words).reshape(g, 128, n, -1)
    if fmt in ("e4m3", "e5m2"):
        vals = words.view(ml_dtypes.float8_e4m3fn if fmt == "e4m3" else ml_dtypes.float8_e5m2).astype(np.float64)
    else:
        nib = np.empty((g, 128, n, 4), np.uint8)
        nib[..., 0::2] = words & 0xF
        nib[..., 1::2] = words >> 4
        vals = E2M1[nib]
    vals = vals * np.repeat(np.exp2(scales.astype(np.float64) - 127.0), 8, axis=1)[..., None]
    return vals.transpose(0, 1, 3, 2).reshape(g * 512, n)


def e4m3fn_bytes(y):
    return np.clip(np.asarray(y, np.float64), -448.0, 448.0).astype(np.float32).astype(ml_dtypes.float8_e4m3fn).view(np.uint8)


def e4m3fn_values(b):
    return np.asarray(b, np.uint8).view(ml_dtypes.float8_e4m3fn).astype(np.float64)


K, V, D, J, N = 512, 512, 512, 256, 256


def setup_inputs():
    n = np.random.standard_normal
    idx = np.random.permutation(V)[:J]
    idx2 = np.random.permutation(D)[:J]
    fk = mx_kscale(K)
    wp = pack_weight(n((K, N)) * 1 / np.sqrt(K) / fk[:, None], "e2m1")
    w2p = pack_weight(n((K, N)) * 1 / np.sqrt(K) / fk[:, None], "e5m2")
    return {
        "ca": e4m3fn_bytes(np.random.randint(-15, 16, (K, V)).astype(np.float64)),
        "cb": e4m3fn_bytes(np.random.randint(-15, 16, (K, V)).astype(np.float64)),
        "cd": e4m3fn_bytes(np.random.randint(-15, 16, (K, D)).astype(np.float64)),
        "ce": e4m3fn_bytes(np.random.randint(-15, 16, (K, D)).astype(np.float64)),
        "sa": (np.random.uniform(0.005, 0.015, (K, 1)) * fk[:, None]).astype(np.float32),
        "sb": (np.random.uniform(0.005, 0.015, (K, 1)) * fk[:, None]).astype(np.float32),
        "w_words": wp[0],
        "w_scales": wp[1],
        "w2_words": w2p[0],
        "w2_scales": w2p[1],
        "offs": striped(idx),
        "offs2": striped(idx2),
    }


def reference(ca, cb, cd, ce, sa, sb, w_words, w_scales, w2_words, w2_scales, offs, offs2):
    idx = unstriped(offs)
    idx2 = unstriped(offs2)
    wu = unpack_weight(w_words, w_scales, "e2m1")
    w2u = unpack_weight(w2_words, w2_scales, "e5m2")
    z1 = (e4m3fn_values(ca)[:, idx] * e4m3fn_values(cd)[:, idx2] - e4m3fn_values(cb)[:, idx] * e4m3fn_values(ce)[:, idx2]) * f64(sa)
    z2 = (e4m3fn_values(ca)[:, idx] * e4m3fn_values(ce)[:, idx2] + e4m3fn_values(cb)[:, idx] * e4m3fn_values(cd)[:, idx2]) * f64(sb)
    z1q = mxq(z1, 0, "e4m3")
    z2q = mxq(z2, 0, "e4m3")
    p = wu.T @ z1q + w2u.T @ z2q
    return p

@@ -1,0 +1,141 @@
+from contextlib import ExitStack
+
+import concourse.mybir as mybir
+
+K, V, J, N = 512, 512, 256, 256
+FLOPS = 2 * 2 * K * N * J
+
+F32 = mybir.dt.float32
+BF16 = mybir.dt.bfloat16
+I32 = mybir.dt.int32
+U32 = mybir.dt.uint32
+U16 = mybir.dt.uint16
+U8 = mybir.dt.uint8
+FP8 = mybir.dt.float8_e4m3fn
+E4M3X4 = mybir.dt.float8_e4m3fn_x4
+E5M2X4 = mybir.dt.float8_e5m2_x4
+E2M1X4 = mybir.dt.float4_e2m1fn_x4
+MULT = mybir.AluOpType.mult
+ADD = mybir.AluOpType.add
+SUB = mybir.AluOpType.subtract
+COPY = mybir.ActivationFunctionType.Copy
+
+P = 128
+PACK = 4
+HALF = J // 2
+
+
+def tile_list_turnedpairs_kernel(tc, ca, cb, cd, ce, sa, sb, w_words, w_scales, w2_words, w2_scales, offs, offs2, out):
+    nc = tc.nc
+    with ExitStack() as ctx:
+        keep = ctx.enter_context(tc.tile_pool(name="keep", bufs=1))
+        psum = ctx.enter_context(tc.psum_pool(name="psum", bufs=1))
+
+        list1 = keep.tile([P, J // 16], U16, name="list1")
+        list2 = keep.tile([P, J // 16], U16, name="list2")
+        step1 = keep.tile([P, PACK], F32, name="step1")
+        step2 = keep.tile([P, PACK], F32, name="step2")
+        w1s = keep.tile([P, N], U8, name="w1s", align_bytes=64)
+        w2s = keep.tile([P, N], U8, name="w2s", align_bytes=64)
+        w1c = keep.tile([P, 2 * N], U8, name="w1c", align_bytes=64)
+        w2c = keep.tile([P, N], U32, name="w2c", align_bytes=64)
+
+        nc.gpsimd.dma_start(step1[:], sa.rearrange("(p t) o -> p (t o)", t=PACK))
+        nc.gpsimd.dma_start(step2[:], sb.rearrange("(p t) o -> p (t o)", t=PACK))
+        nc.vector.memset(w1s[:].bitcast(I32), 0)
+        nc.vector.memset(w2s[:].bitcast(I32), 0)
+
+        def load_plane(name, table, t):
+            rows = keep.tile([P, V], U8, name="%s_rows%d" % (name, t))
+            nc.sync.dma_start(rows[:], table.rearrange("(p t) v -> t p v", t=PACK)[t])
+            return rows
+
+        nc.sync.dma_start(list2[:], offs2)
+        rows_d = [load_plane("d", cd, t) for t in range(PACK)]
+        rows_e = [load_plane("e", ce, t) for t in range(PACK)]
+        nc.sync.dma_start(list1[:], offs)
+        rows_a = [load_plane("a", ca, t) for t in range(PACK)]
+        rows_b = [load_plane("b", cb, t) for t in range(PACK)]
+        nc.sync.dma_start(w1c[:].bitcast(I32), w_words[0].bitcast(I32))
+        nc.sync.dma_start(w2c[:].bitcast(I32), w2_words[0].rearrange("p n t -> p (n t)").bitcast(I32))
+        for q in range(4):
+            nc.sync.dma_start(w1s[32 * q : 32 * q + 4, :].bitcast(I32), w_scales[0, 4 * q : 4 * q + 4, :].bitcast(I32))
+        for q in range(4):
+            nc.sync.dma_start(w2s[32 * q : 32 * q + 4, :].bitcast(I32), w2_scales[0, 4 * q : 4 * q + 4, :].bitcast(I32))
+
+        ga = keep.tile([P, PACK * J], U8, name="ga")
+        gb = keep.tile([P, PACK * J], U8, name="gb")
+        gd = keep.tile([P, PACK * J], U8, name="gd")
+        ge = keep.tile([P, PACK * J], U8, name="ge")
+        d1 = keep.tile([P, PACK * J], F32, name="d1")
+        d2 = keep.tile([P, PACK * J], F32, name="d2")
+        e1 = keep.tile([P, PACK * J], F32, name="e1")
+        e2 = keep.tile([P, PACK * J], F32, name="e2")
+
+        def plane(t):
+            return slice(t * J, (t + 1) * J)
+
+        for picked, rows, by1, by2 in ((gd, rows_d, d1, d2), (ge, rows_e, e1, e2)):
+            for t in range(PACK):
+                nc.vector.tensor_copy(picked[:, plane(t)], rows[t][:].indirect(list2[:]))
+                codes = picked[:, plane(t)].bitcast(FP8)
+                nc.scalar.activation(by1[:, plane(t)], codes, COPY, scale=step1[:, t : t + 1])
+                nc.scalar.activation(by2[:, plane(t)], codes, COPY, scale=step2[:, t : t + 1])
+        for picked, rows in ((ga, rows_a), (gb, rows_b)):
+            for t in range(PACK):
+                nc.vector.tensor_copy(picked[:, plane(t)], rows[t][:].indirect(list1[:]))
+
+        ad = keep.tile([P, PACK * J], F32, name="ad")
+        ae = keep.tile([P, PACK * J], F32, name="ae")
+        be = keep.tile([P, PACK * J], F32, name="be")
+        bd = keep.tile([P, PACK * J], F32, name="bd")
+        nc.vector.tensor_tensor(ad[:], ga[:].bitcast(FP8), d1[:], MULT)
+        nc.vector.tensor_tensor(ae[:], ga[:].bitcast(FP8), e2[:], MULT)
+        nc.vector.tensor_tensor(be[:], gb[:].bitcast(FP8), e1[:], MULT)
+        nc.vector.tensor_tensor(bd[:], gb[:].bitcast(FP8), d2[:], MULT)
+
+        def woven(tile, h):
+            return tile[:].rearrange("p (t h c i) -> p h c t i", t=PACK, h=2, i=2)[:, h]
+
+        z, zc, zs = {}, {}, {}
+        for h in range(2):
+            for part in range(2):
+                z[part, h] = keep.tile([P, HALF * PACK], BF16, name="z%d_%d" % (part, h), align_bytes=64)
+                zc[part, h] = keep.tile([P, HALF], U32, name="zc%d_%d" % (part, h), align_bytes=64)
+                zs[part, h] = keep.tile([P, HALF], U8, name="zs%d_%d" % (part, h), align_bytes=64)
+
+        def combine(part, h):
+            dst = z[part, h][:].rearrange("p (c i t) -> p c t i", t=PACK, i=2)
+            if part == 0:
+                nc.vector.tensor_tensor(dst, woven(ad, h), woven(be, h), SUB)
+            else:
+                nc.vector.tensor_tensor(dst, woven(ae, h), woven(bd, h), ADD)
+
+        def quantise(part, h):
+            nc.vector.quantize_mx(zc[part, h][:].bitcast(E4M3X4), zs[part, h][:], z[part, h][:])
+
+        def multiply(h):
+            res = keep.tile([P, 2, HALF], F32, name="res%d" % h)
+            for m in range(2):
+                acc = psum.tile([P, HALF], F32, name="acc%d_%d" % (h, m))
+                cols = slice(m * P, (m + 1) * P)
+                nc.tensor.matmul_mx(acc[:], lhsT=w1c[:, 2 * m * P : 2 * (m + 1) * P].bitcast(E2M1X4), lhsT_scale=w1s[:, cols],
+                                    rhs=zc[0, h][:].bitcast(E4M3X4), rhs_scale=zs[0, h][:], start=True, stop=False)
+                nc.tensor.matmul_mx(acc[:], lhsT=w2c[:, cols].bitcast(E5M2X4), lhsT_scale=w2s[:, cols],
+                                    rhs=zc[1, h][:].bitcast(E4M3X4), rhs_scale=zs[1, h][:], start=False, stop=True)
+                if h == 1 and m == 1:
+                    nc.vector.tensor_copy(res[:, m, :], acc[:])
+                else:
+                    nc.scalar.copy(res[:, m, :], acc[:])
+            nc.sync.dma_start(out.rearrange("(m p) j -> p m j", p=P)[:, :, h * HALF : (h + 1) * HALF], res[:])
+
+        combine(0, 0)
+        combine(1, 0)
+        quantise(0, 0)
+        combine(0, 1)
+        quantise(1, 0)
+        multiply(0)
+        combine(1, 1)
+        quantise(0, 1)
+        quantise(1, 1)
+        multiply(1)

@@ -23,6 +23,7 @@ COPY = mybir.ActivationFunctionType.Copy
 P = 128
 PACK = 4
 HALF = J // 2
+GP_PLANES = 3
 
 
 def tile_list_turnedpairs_kernel(tc, ca, cb, cd, ce, sa, sb, w_words, w_scales, w2_words, w2_scales, offs, offs2, out):
@@ -40,22 +41,27 @@ def tile_list_turnedpairs_kernel(tc, ca, cb, cd, ce, sa, sb, w_words, w_scales, 
         w1c = keep.tile([P, 2 * N], U8, name="w1c", align_bytes=64)
         w2c = keep.tile([P, N], U32, name="w2c", align_bytes=64)
 
-        nc.gpsimd.dma_start(step1[:], sa.rearrange("(p t) o -> p (t o)", t=PACK))
-        nc.gpsimd.dma_start(step2[:], sb.rearrange("(p t) o -> p (t o)", t=PACK))
         nc.vector.memset(w1s[:].bitcast(I32), 0)
         nc.vector.memset(w2s[:].bitcast(I32), 0)
 
-        def load_plane(name, table, t):
-            rows = keep.tile([P, V], U8, name="%s_rows%d" % (name, t))
-            nc.sync.dma_start(rows[:], table.rearrange("(p t) v -> t p v", t=PACK)[t])
-            return rows
+        rows = {}
 
+        def load_plane(name, table, t):
+            rows[name, t] = keep.tile([P, V], U8, name="%s_rows%d" % (name, t))
+            nc.sync.dma_start(rows[name, t][:], table.rearrange("(p t) v -> t p v", t=PACK)[t])
+
+        load_plane("d", cd, 0)
         nc.sync.dma_start(list2[:], offs2)
-        rows_d = [load_plane("d", cd, t) for t in range(PACK)]
-        rows_e = [load_plane("e", ce, t) for t in range(PACK)]
+        load_plane("a", ca, 0)
         nc.sync.dma_start(list1[:], offs)
-        rows_a = [load_plane("a", ca, t) for t in range(PACK)]
-        rows_b = [load_plane("b", cb, t) for t in range(PACK)]
+        nc.scalar.dma_start(step1[:], sa.rearrange("(p t) o -> p (t o)", t=PACK))
+        nc.scalar.dma_start(step2[:], sb.rearrange("(p t) o -> p (t o)", t=PACK))
+        load_plane("e", ce, 0)
+        load_plane("b", cb, 0)
+        for t in range(1, PACK):
+            order = "daeb" if t < GP_PLANES else "deab"
+            for name in order:
+                load_plane(name, {"a": ca, "b": cb, "d": cd, "e": ce}[name], t)
         nc.sync.dma_start(w1c[:].bitcast(I32), w_words[0].bitcast(I32))
         nc.sync.dma_start(w2c[:].bitcast(I32), w2_words[0].rearrange("p n t -> p (n t)").bitcast(I32))
         for q in range(4):
@@ -63,39 +69,56 @@ def tile_list_turnedpairs_kernel(tc, ca, cb, cd, ce, sa, sb, w_words, w_scales, 
         for q in range(4):
             nc.sync.dma_start(w2s[32 * q : 32 * q + 4, :].bitcast(I32), w2_scales[0, 4 * q : 4 * q + 4, :].bitcast(I32))
 
-        ga = keep.tile([P, PACK * J], U8, name="ga")
-        gb = keep.tile([P, PACK * J], U8, name="gb")
-        gd = keep.tile([P, PACK * J], U8, name="gd")
-        ge = keep.tile([P, PACK * J], U8, name="ge")
-        d1 = keep.tile([P, PACK * J], F32, name="d1")
-        d2 = keep.tile([P, PACK * J], F32, name="d2")
-        e1 = keep.tile([P, PACK * J], F32, name="e1")
-        e2 = keep.tile([P, PACK * J], F32, name="e2")
+        with_a = keep.tile([P, PACK, 2, J], F32, name="with_a")
+        with_b = keep.tile([P, PACK, 2, J], F32, name="with_b")
 
-        def plane(t):
-            return slice(t * J, (t + 1) * J)
+        def gather(name, t, offsets):
+            picked = keep.tile([P, J], U8, name="%s_picked%d" % (name, t))
+            nc.vector.tensor_copy(picked[:], rows[name, t][:].indirect(offsets[:]))
+            return picked[:].bitcast(FP8)
 
-        for picked, rows, by1, by2 in ((gd, rows_d, d1, d2), (ge, rows_e, e1, e2)):
-            for t in range(PACK):
-                nc.vector.tensor_copy(picked[:, plane(t)], rows[t][:].indirect(list2[:]))
-                codes = picked[:, plane(t)].bitcast(FP8)
-                nc.scalar.activation(by1[:, plane(t)], codes, COPY, scale=step1[:, t : t + 1])
-                nc.scalar.activation(by2[:, plane(t)], codes, COPY, scale=step2[:, t : t + 1])
-        for picked, rows in ((ga, rows_a), (gb, rows_b)):
-            for t in range(PACK):
-                nc.vector.tensor_copy(picked[:, plane(t)], rows[t][:].indirect(list1[:]))
+        late = []
+        for t in range(PACK):
+            for_a = keep.tile([P, 2, J], F32, name="for_a%d" % t)
+            for_b = keep.tile([P, 2, J], F32, name="for_b%d" % t)
+            s1, s2 = step1[:, t : t + 1], step2[:, t : t + 1]
+            on_gpsimd = t < GP_PLANES
+            d = gather("d", t, list2)
+            nc.scalar.activation(for_a[:, 0, :], d, COPY, scale=s1)
+            if on_gpsimd:
+                a = gather("a", t, list1)
+                a32 = keep.tile([P, J], F32, name="a32_%d" % t)
+                nc.scalar.copy(a32[:], a)
+                if t == 0:
+                    nc.gpsimd.tensor_tensor(with_a[:, t, 0, :], a32[:], for_a[:, 0, :], MULT)
+                nc.scalar.activation(for_b[:, 1, :], d, COPY, scale=s2)
+                e = gather("e", t, list2)
+                nc.scalar.activation(for_a[:, 1, :], e, COPY, scale=s2)
+                if t == 0:
+                    nc.gpsimd.tensor_tensor(with_a[:, t, 1, :], a32[:], for_a[:, 1, :], MULT)
+                else:
+                    nc.gpsimd.tensor_tensor(with_a[:, t], a32[:].unsqueeze(1).to_broadcast([P, 2, J]), for_a[:], MULT)
+                nc.scalar.activation(for_b[:, 0, :], e, COPY, scale=s1)
+                b = gather("b", t, list1)
+                b32 = keep.tile([P, J], F32, name="b32_%d" % t)
+                nc.scalar.copy(b32[:], b)
+                nc.gpsimd.tensor_tensor(with_b[:, t], b32[:].unsqueeze(1).to_broadcast([P, 2, J]), for_b[:], MULT)
+            else:
+                nc.scalar.activation(for_b[:, 1, :], d, COPY, scale=s2)
+                e = gather("e", t, list2)
+                nc.scalar.activation(for_a[:, 1, :], e, COPY, scale=s2)
+                nc.scalar.activation(for_b[:, 0, :], e, COPY, scale=s1)
+                a = gather("a", t, list1)
+                b = gather("b", t, list1)
+                late.append((t, a, b, for_a, for_b))
+        for t, a, b, for_a, for_b in late:
+            for part in range(2):
+                nc.vector.tensor_tensor(with_a[:, t, part, :], a, for_a[:, part, :], MULT)
+            for part in range(2):
+                nc.vector.tensor_tensor(with_b[:, t, part, :], b, for_b[:, part, :], MULT)
 
-        ad = keep.tile([P, PACK * J], F32, name="ad")
-        ae = keep.tile([P, PACK * J], F32, name="ae")
-        be = keep.tile([P, PACK * J], F32, name="be")
-        bd = keep.tile([P, PACK * J], F32, name="bd")
-        nc.vector.tensor_tensor(ad[:], ga[:].bitcast(FP8), d1[:], MULT)
-        nc.vector.tensor_tensor(ae[:], ga[:].bitcast(FP8), e2[:], MULT)
-        nc.vector.tensor_tensor(be[:], gb[:].bitcast(FP8), e1[:], MULT)
-        nc.vector.tensor_tensor(bd[:], gb[:].bitcast(FP8), d2[:], MULT)
-
-        def woven(tile, h):
-            return tile[:].rearrange("p (t h c i) -> p h c t i", t=PACK, h=2, i=2)[:, h]
+        def woven(tile, part, h):
+            return tile[:, :, part, h * HALF : (h + 1) * HALF].rearrange("p t (c i) -> p c t i", i=2)
 
         z, zc, zs = {}, {}, {}
         for h in range(2):
@@ -106,10 +129,7 @@ def tile_list_turnedpairs_kernel(tc, ca, cb, cd, ce, sa, sb, w_words, w_scales, 
 
         def combine(part, h):
             dst = z[part, h][:].rearrange("p (c i t) -> p c t i", t=PACK, i=2)
-            if part == 0:
-                nc.vector.tensor_tensor(dst, woven(ad, h), woven(be, h), SUB)
-            else:
-                nc.vector.tensor_tensor(dst, woven(ae, h), woven(bd, h), ADD)
+            nc.vector.tensor_tensor(dst, woven(with_a, part, h), woven(with_b, part, h), ADD if part else SUB)
 
         def quantise(part, h):
             nc.vector.quantize_mx(zc[part, h][:].bitcast(E4M3X4), zs[part, h][:], z[part, h][:])

@@ -23,11 +23,11 @@ COPY = mybir.ActivationFunctionType.Copy
 P = 128
 PACK = 4
 HALF = J // 2
-GP_PLANES = 3
 
 
 def tile_list_turnedpairs_kernel(tc, ca, cb, cd, ce, sa, sb, w_words, w_scales, w2_words, w2_scales, offs, offs2, out):
     nc = tc.nc
+    tables = {"a": ca, "b": cb, "d": cd, "e": ce}
     with ExitStack() as ctx:
         keep = ctx.enter_context(tc.tile_pool(name="keep", bufs=1))
         psum = ctx.enter_context(tc.psum_pool(name="psum", bufs=1))
@@ -44,24 +44,18 @@ def tile_list_turnedpairs_kernel(tc, ca, cb, cd, ce, sa, sb, w_words, w_scales, 
         nc.vector.memset(w1s[:].bitcast(I32), 0)
         nc.vector.memset(w2s[:].bitcast(I32), 0)
 
+        order = [(name, t) for t in range(2) for name in "daeb"]
+        order = order + [("d", 2), ("a", 2), ("e", 2), ("d", 3), ("e", 3), ("a", 3), ("b", 2), ("b", 3)]
         rows = {}
-
-        def load_plane(name, table, t):
+        for name, t in order:
             rows[name, t] = keep.tile([P, V], U8, name="%s_rows%d" % (name, t))
-            nc.sync.dma_start(rows[name, t][:], table.rearrange("(p t) v -> t p v", t=PACK)[t])
-
-        load_plane("d", cd, 0)
-        nc.sync.dma_start(list2[:], offs2)
-        load_plane("a", ca, 0)
-        nc.sync.dma_start(list1[:], offs)
-        nc.scalar.dma_start(step1[:], sa.rearrange("(p t) o -> p (t o)", t=PACK))
-        nc.scalar.dma_start(step2[:], sb.rearrange("(p t) o -> p (t o)", t=PACK))
-        load_plane("e", ce, 0)
-        load_plane("b", cb, 0)
-        for t in range(1, PACK):
-            order = "daeb" if t < GP_PLANES else "deab"
-            for name in order:
-                load_plane(name, {"a": ca, "b": cb, "d": cd, "e": ce}[name], t)
+            nc.sync.dma_start(rows[name, t][:], tables[name].rearrange("(p t) v -> t p v", t=PACK)[t])
+            if (name, t) == ("d", 0):
+                nc.sync.dma_start(list2[:], offs2)
+            if (name, t) == ("a", 0):
+                nc.sync.dma_start(list1[:], offs)
+                nc.scalar.dma_start(step1[:], sa.rearrange("(p t) o -> p (t o)", t=PACK))
+                nc.scalar.dma_start(step2[:], sb.rearrange("(p t) o -> p (t o)", t=PACK))
         nc.sync.dma_start(w1c[:].bitcast(I32), w_words[0].bitcast(I32))
         nc.sync.dma_start(w2c[:].bitcast(I32), w2_words[0].rearrange("p n t -> p (n t)").bitcast(I32))
         for q in range(4):
@@ -69,56 +63,63 @@ def tile_list_turnedpairs_kernel(tc, ca, cb, cd, ce, sa, sb, w_words, w_scales, 
         for q in range(4):
             nc.sync.dma_start(w2s[32 * q : 32 * q + 4, :].bitcast(I32), w2_scales[0, 4 * q : 4 * q + 4, :].bitcast(I32))
 
-        with_a = keep.tile([P, PACK, 2, J], F32, name="with_a")
-        with_b = keep.tile([P, PACK, 2, J], F32, name="with_b")
+        products = {name: keep.tile([P, PACK, 2, J], F32, name="times_" + name) for name in "ab"}
+        factors = {(name, t): keep.tile([P, 2, J], F32, name="for_%s%d" % (name, t))[:]
+                   for name in "ab" for t in range(PACK) if (name, t) != ("a", 2)}
+        factors["a", 2] = products["b"][:, 2]
+        wide = {(name, t): keep.tile([P, J], F32, name="%s_wide%d" % (name, t))[:] for name in "ab" for t in range(2)}
+        wide["a", 2] = products["a"][:, 3].rearrange("p z j -> p (z j)")[:, HALF : HALF + J]
+        codes = {}
 
-        def gather(name, t, offsets):
+        def gather(name, t):
             picked = keep.tile([P, J], U8, name="%s_picked%d" % (name, t))
-            nc.vector.tensor_copy(picked[:], rows[name, t][:].indirect(offsets[:]))
-            return picked[:].bitcast(FP8)
+            nc.vector.tensor_copy(picked[:], rows[name, t][:].indirect((list1 if name in "ab" else list2)[:]))
+            codes[name, t] = picked[:].bitcast(FP8)
 
-        late = []
-        for t in range(PACK):
-            for_a = keep.tile([P, 2, J], F32, name="for_a%d" % t)
-            for_b = keep.tile([P, 2, J], F32, name="for_b%d" % t)
-            s1, s2 = step1[:, t : t + 1], step2[:, t : t + 1]
-            on_gpsimd = t < GP_PLANES
-            d = gather("d", t, list2)
-            nc.scalar.activation(for_a[:, 0, :], d, COPY, scale=s1)
-            if on_gpsimd:
-                a = gather("a", t, list1)
-                a32 = keep.tile([P, J], F32, name="a32_%d" % t)
-                nc.scalar.copy(a32[:], a)
-                if t == 0:
-                    nc.gpsimd.tensor_tensor(with_a[:, t, 0, :], a32[:], for_a[:, 0, :], MULT)
-                nc.scalar.activation(for_b[:, 1, :], d, COPY, scale=s2)
-                e = gather("e", t, list2)
-                nc.scalar.activation(for_a[:, 1, :], e, COPY, scale=s2)
-                if t == 0:
-                    nc.gpsimd.tensor_tensor(with_a[:, t, 1, :], a32[:], for_a[:, 1, :], MULT)
-                else:
-                    nc.gpsimd.tensor_tensor(with_a[:, t], a32[:].unsqueeze(1).to_broadcast([P, 2, J]), for_a[:], MULT)
-                nc.scalar.activation(for_b[:, 0, :], e, COPY, scale=s1)
-                b = gather("b", t, list1)
-                b32 = keep.tile([P, J], F32, name="b32_%d" % t)
-                nc.scalar.copy(b32[:], b)
-                nc.gpsimd.tensor_tensor(with_b[:, t], b32[:].unsqueeze(1).to_broadcast([P, 2, J]), for_b[:], MULT)
-            else:
-                nc.scalar.activation(for_b[:, 1, :], d, COPY, scale=s2)
-                e = gather("e", t, list2)
-                nc.scalar.activation(for_a[:, 1, :], e, COPY, scale=s2)
-                nc.scalar.activation(for_b[:, 0, :], e, COPY, scale=s1)
-                a = gather("a", t, list1)
-                b = gather("b", t, list1)
-                late.append((t, a, b, for_a, for_b))
-        for t, a, b, for_a, for_b in late:
-            for part in range(2):
-                nc.vector.tensor_tensor(with_a[:, t, part, :], a, for_a[:, part, :], MULT)
-            for part in range(2):
-                nc.vector.tensor_tensor(with_b[:, t, part, :], b, for_b[:, part, :], MULT)
+        def factor(name, t, part):
+            source = "de"[part] if name == "a" else "ed"[part]
+            step = (step1, step2)[part]
+            nc.scalar.activation(factors[name, t][:, part, :], codes[source, t], COPY, scale=step[:, t : t + 1])
 
-        def woven(tile, part, h):
-            return tile[:, :, part, h * HALF : (h + 1) * HALF].rearrange("p t (c i) -> p c t i", i=2)
+        def widen(name, t):
+            nc.scalar.copy(wide[name, t], codes[name, t])
+
+        def on_gpsimd(name, t, parts):
+            spread = wide[name, t].unsqueeze(1).to_broadcast([P, parts.stop - parts.start, J])
+            nc.gpsimd.tensor_tensor(products[name][:, t, parts, :], spread, factors[name, t][:, parts, :], MULT)
+
+        for t in range(3):
+            gather("d", t)
+            factor("a", t, 0)
+            gather("a", t)
+            widen("a", t)
+            if t == 0:
+                on_gpsimd("a", t, slice(0, 1))
+            gather("e", t)
+            factor("a", t, 1)
+            on_gpsimd("a", t, slice(1 if t == 0 else 0, 2))
+            if t < 2:
+                factor("b", t, 1)
+                factor("b", t, 0)
+                gather("b", t)
+                widen("b", t)
+                on_gpsimd("b", t, slice(0, 2))
+        gather("d", 3)
+        factor("a", 3, 0)
+        gather("e", 3)
+        factor("a", 3, 1)
+        for t in (2, 3):
+            for part in range(2):
+                factor("b", t, part)
+        on_vector = [("a", 3), ("b", 2), ("b", 3)]
+        for name, t in on_vector:
+            gather(name, t)
+        for name, t in on_vector:
+            for part in range(2):
+                nc.vector.tensor_tensor(products[name][:, t, part, :], codes[name, t], factors[name, t][:, part, :], MULT)
+
+        def woven(name, part, h):
+            return products[name][:, :, part, h * HALF : (h + 1) * HALF].rearrange("p t (c i) -> p c t i", i=2)
 
         z, zc, zs = {}, {}, {}
         for h in range(2):
@@ -129,33 +130,43 @@ def tile_list_turnedpairs_kernel(tc, ca, cb, cd, ce, sa, sb, w_words, w_scales, 
 
         def combine(part, h):
             dst = z[part, h][:].rearrange("p (c i t) -> p c t i", t=PACK, i=2)
-            nc.vector.tensor_tensor(dst, woven(with_a, part, h), woven(with_b, part, h), ADD if part else SUB)
+            nc.vector.tensor_tensor(dst, woven("a", part, h), woven("b", part, h), ADD if part else SUB)
 
         def quantise(part, h):
             nc.vector.quantize_mx(zc[part, h][:].bitcast(E4M3X4), zs[part, h][:], z[part, h][:])
 
-        def multiply(h):
-            res = keep.tile([P, 2, HALF], F32, name="res%d" % h)
+        acc = {(h, m): psum.tile([P, HALF], F32, name="acc%d_%d" % (h, m)) for h in range(2) for m in range(2)}
+
+        def multiply(part, h):
             for m in range(2):
-                acc = psum.tile([P, HALF], F32, name="acc%d_%d" % (h, m))
                 cols = slice(m * P, (m + 1) * P)
-                nc.tensor.matmul_mx(acc[:], lhsT=w1c[:, 2 * m * P : 2 * (m + 1) * P].bitcast(E2M1X4), lhsT_scale=w1s[:, cols],
-                                    rhs=zc[0, h][:].bitcast(E4M3X4), rhs_scale=zs[0, h][:], start=True, stop=False)
-                nc.tensor.matmul_mx(acc[:], lhsT=w2c[:, cols].bitcast(E5M2X4), lhsT_scale=w2s[:, cols],
-                                    rhs=zc[1, h][:].bitcast(E4M3X4), rhs_scale=zs[1, h][:], start=False, stop=True)
-                if h == 1 and m == 1:
-                    nc.vector.tensor_copy(res[:, m, :], acc[:])
+                if part == 0:
+                    weights, scales = w1c[:, 2 * m * P : 2 * (m + 1) * P].bitcast(E2M1X4), w1s[:, cols]
                 else:
-                    nc.scalar.copy(res[:, m, :], acc[:])
+                    weights, scales = w2c[:, cols].bitcast(E5M2X4), w2s[:, cols]
+                nc.tensor.matmul_mx(acc[h, m][:], lhsT=weights, lhsT_scale=scales, rhs=zc[part, h][:].bitcast(E4M3X4),
+                                    rhs_scale=zs[part, h][:], start=part == 0, stop=part == 1)
+
+        def store(h):
+            res = keep.tile([P, 2, HALF], F32, name="res%d" % h)
+            nc.scalar.copy(res[:, 0, :], acc[h, 0][:])
+            if h == 0:
+                nc.scalar.copy(res[:, 1, :], acc[h, 1][:])
+            else:
+                nc.vector.tensor_copy(res[:, 1, :], acc[h, 1][:])
             nc.sync.dma_start(out.rearrange("(m p) j -> p m j", p=P)[:, :, h * HALF : (h + 1) * HALF], res[:])
 
         combine(0, 0)
         combine(1, 0)
         quantise(0, 0)
+        multiply(0, 0)
         combine(0, 1)
         quantise(1, 0)
-        multiply(0)
+        multiply(1, 0)
+        store(0)
         combine(1, 1)
         quantise(0, 1)
+        multiply(0, 1)
         quantise(1, 1)
-        multiply(1)
+        multiply(1, 1)
+        store(1)

@@ -44,8 +44,9 @@ def tile_list_turnedpairs_kernel(tc, ca, cb, cd, ce, sa, sb, w_words, w_scales, 
         nc.vector.memset(w1s[:].bitcast(I32), 0)
         nc.vector.memset(w2s[:].bitcast(I32), 0)
 
-        order = [(name, t) for t in range(2) for name in "daeb"]
-        order = order + [("d", 2), ("a", 2), ("e", 2), ("d", 3), ("e", 3), ("a", 3), ("b", 2), ("b", 3)]
+        nc.gpsimd.dma_start(step2[:], sb.rearrange("(p t) o -> p (t o)", t=PACK))
+        nc.scalar.dma_start(step1[:], sa.rearrange("(p t) o -> p (t o)", t=PACK))
+        order = [(name, t) for t in range(3) for name in "daeb"] + [(name, 3) for name in "deab"]
         rows = {}
         for name, t in order:
             rows[name, t] = keep.tile([P, V], U8, name="%s_rows%d" % (name, t))
@@ -54,8 +55,6 @@ def tile_list_turnedpairs_kernel(tc, ca, cb, cd, ce, sa, sb, w_words, w_scales, 
                 nc.sync.dma_start(list2[:], offs2)
             if (name, t) == ("a", 0):
                 nc.sync.dma_start(list1[:], offs)
-                nc.scalar.dma_start(step1[:], sa.rearrange("(p t) o -> p (t o)", t=PACK))
-                nc.scalar.dma_start(step2[:], sb.rearrange("(p t) o -> p (t o)", t=PACK))
         nc.sync.dma_start(w1c[:].bitcast(I32), w_words[0].bitcast(I32))
         nc.sync.dma_start(w2c[:].bitcast(I32), w2_words[0].rearrange("p n t -> p (n t)").bitcast(I32))
         for q in range(4):
@@ -63,30 +62,43 @@ def tile_list_turnedpairs_kernel(tc, ca, cb, cd, ce, sa, sb, w_words, w_scales, 
         for q in range(4):
             nc.sync.dma_start(w2s[32 * q : 32 * q + 4, :].bitcast(I32), w2_scales[0, 4 * q : 4 * q + 4, :].bitcast(I32))
 
-        products = {name: keep.tile([P, PACK, 2, J], F32, name="times_" + name) for name in "ab"}
+        times_a = keep.tile([P, PACK, 2, J], F32, name="times_a")
+        times_b = keep.tile([P, 2, PACK, J], F32, name="times_b")
+        products = {"a": times_a[:].rearrange("p t z j -> p z t j"), "b": times_b[:]}
         factors = {(name, t): keep.tile([P, 2, J], F32, name="for_%s%d" % (name, t))[:]
-                   for name in "ab" for t in range(PACK) if (name, t) != ("a", 2)}
-        factors["a", 2] = products["b"][:, 2]
-        wide = {(name, t): keep.tile([P, J], F32, name="%s_wide%d" % (name, t))[:] for name in "ab" for t in range(2)}
-        wide["a", 2] = products["a"][:, 3].rearrange("p z j -> p (z j)")[:, HALF : HALF + J]
-        codes = {}
+                   for name in "ab" for t in range(PACK) if name == "a" or t < 2}
+        late_factors = keep.tile([P, 2, J], F32, name="late_factors")
+        late_b = keep.tile([P, 2 * J], U8, name="b_picked_late")
+        codes, wide = {}, {}
+
+        def factor_of(name, t, part):
+            if name == "b" and t >= 2:
+                return late_factors[:, t - 2, :] if part == 0 else times_a[:, 3, t - 2, :]
+            return factors[name, t][:, part, :]
 
         def gather(name, t):
-            picked = keep.tile([P, J], U8, name="%s_picked%d" % (name, t))
-            nc.vector.tensor_copy(picked[:], rows[name, t][:].indirect((list1 if name in "ab" else list2)[:]))
-            codes[name, t] = picked[:].bitcast(FP8)
+            if name == "b" and t >= 2:
+                picked = late_b[:, (t - 2) * J : (t - 1) * J]
+            else:
+                picked = keep.tile([P, J], U8, name="%s_picked%d" % (name, t))[:]
+            nc.vector.tensor_copy(picked, rows[name, t][:].indirect((list1 if name in "ab" else list2)[:]))
+            codes[name, t] = picked.bitcast(FP8)
 
         def factor(name, t, part):
             source = "de"[part] if name == "a" else "ed"[part]
             step = (step1, step2)[part]
-            nc.scalar.activation(factors[name, t][:, part, :], codes[source, t], COPY, scale=step[:, t : t + 1])
+            nc.scalar.activation(factor_of(name, t, part), codes[source, t], COPY, scale=step[:, t : t + 1])
 
         def widen(name, t):
-            nc.scalar.copy(wide[name, t], codes[name, t])
+            wide[name, t] = keep.tile([P, J], F32, name="%s_wide%d" % (name, t))
+            nc.scalar.copy(wide[name, t][:], codes[name, t])
 
-        def on_gpsimd(name, t, parts):
-            spread = wide[name, t].unsqueeze(1).to_broadcast([P, parts.stop - parts.start, J])
-            nc.gpsimd.tensor_tensor(products[name][:, t, parts, :], spread, factors[name, t][:, parts, :], MULT)
+        def on_gpsimd(name, t, part):
+            nc.gpsimd.tensor_tensor(products[name][:, part, t, :], wide[name, t][:], factor_of(name, t, part), MULT)
+
+        def both_on_gpsimd(name, t):
+            spread = wide[name, t][:].unsqueeze(1).to_broadcast([P, 2, J])
+            nc.gpsimd.tensor_tensor(products[name][:, :, t, :], spread, factors[name, t], MULT)
 
         for t in range(3):
             gather("d", t)
@@ -94,32 +106,39 @@ def tile_list_turnedpairs_kernel(tc, ca, cb, cd, ce, sa, sb, w_words, w_scales, 
             gather("a", t)
             widen("a", t)
             if t == 0:
-                on_gpsimd("a", t, slice(0, 1))
+                on_gpsimd("a", t, 0)
             gather("e", t)
             factor("a", t, 1)
-            on_gpsimd("a", t, slice(1 if t == 0 else 0, 2))
+            if t == 0:
+                on_gpsimd("a", t, 1)
+            else:
+                both_on_gpsimd("a", t)
             if t < 2:
-                factor("b", t, 1)
                 factor("b", t, 0)
+                factor("b", t, 1)
                 gather("b", t)
                 widen("b", t)
-                on_gpsimd("b", t, slice(0, 2))
+                both_on_gpsimd("b", t)
+        factor("b", 2, 0)
+        gather("b", 2)
+        widen("b", 2)
+        on_gpsimd("b", 2, 0)
         gather("d", 3)
-        factor("a", 3, 0)
         gather("e", 3)
+        factor("b", 2, 1)
+        factor("b", 3, 1)
+        factor("b", 3, 0)
+        factor("a", 3, 0)
         factor("a", 3, 1)
-        for t in (2, 3):
-            for part in range(2):
-                factor("b", t, part)
-        on_vector = [("a", 3), ("b", 2), ("b", 3)]
-        for name, t in on_vector:
-            gather(name, t)
-        for name, t in on_vector:
-            for part in range(2):
-                nc.vector.tensor_tensor(products[name][:, t, part, :], codes[name, t], factors[name, t][:, part, :], MULT)
+        gather("a", 3)
+        gather("b", 3)
+        nc.vector.tensor_tensor(products["b"][:, 1, 2:4, :].rearrange("p t j -> p (t j)"), late_b[:].bitcast(FP8), times_a[:, 3].rearrange("p z j -> p (z j)"), MULT)
+        nc.vector.tensor_tensor(products["b"][:, 0, 3, :], codes["b", 3], factor_of("b", 3, 0), MULT)
+        for part in range(2):
+            nc.vector.tensor_tensor(products["a"][:, part, 3, :], codes["a", 3], factors["a", 3][:, part, :], MULT)
 
         def woven(name, part, h):
-            return products[name][:, :, part, h * HALF : (h + 1) * HALF].rearrange("p t (c i) -> p c t i", i=2)
+            return products[name][:, part, :, h * HALF : (h + 1) * HALF].rearrange("p t (c i) -> p c t i", i=2)
 
         z, zc, zs = {}, {}, {}
         for h in range(2):

@@ -1,6 +1,7 @@
 from contextlib import ExitStack
 
 import concourse.mybir as mybir
+from concourse.masks import make_identity
 
 K, V, J, N = 512, 512, 256, 256
 FLOPS = 2 * 2 * K * N * J
@@ -17,12 +18,12 @@ E5M2X4 = mybir.dt.float8_e5m2_x4
 E2M1X4 = mybir.dt.float4_e2m1fn_x4
 MULT = mybir.AluOpType.mult
 ADD = mybir.AluOpType.add
-SUB = mybir.AluOpType.subtract
 COPY = mybir.ActivationFunctionType.Copy
 
 P = 128
 PACK = 4
 HALF = J // 2
+EARLY = 2
 
 
 def tile_list_turnedpairs_kernel(tc, ca, cb, cd, ce, sa, sb, w_words, w_scales, w2_words, w2_scales, offs, offs2, out):
@@ -36,17 +37,23 @@ def tile_list_turnedpairs_kernel(tc, ca, cb, cd, ce, sa, sb, w_words, w_scales, 
         list2 = keep.tile([P, J // 16], U16, name="list2")
         step1 = keep.tile([P, PACK], F32, name="step1")
         step2 = keep.tile([P, PACK], F32, name="step2")
-        w1s = keep.tile([P, N], U8, name="w1s", align_bytes=64)
-        w2s = keep.tile([P, N], U8, name="w2s", align_bytes=64)
-        w1c = keep.tile([P, 2 * N], U8, name="w1c", align_bytes=64)
-        w2c = keep.tile([P, N], U32, name="w2c", align_bytes=64)
+        w1_scale_rows = keep.tile([P, N], U8, name="w1_scale_rows", align_bytes=64)
+        w2_scale_rows = keep.tile([P, N], U8, name="w2_scale_rows", align_bytes=64)
+        w1_codes = keep.tile([P, 2 * N], U8, name="w1_codes", align_bytes=64)
+        w2_codes = keep.tile([P, N], U32, name="w2_codes", align_bytes=64)
 
-        nc.vector.memset(w1s[:].bitcast(I32), 0)
-        nc.vector.memset(w2s[:].bitcast(I32), 0)
+        nc.vector.memset(w1_scale_rows[:].bitcast(I32), 0)
+        nc.vector.memset(w2_scale_rows[:].bitcast(I32), 0)
 
         nc.gpsimd.dma_start(step2[:], sb.rearrange("(p t) o -> p (t o)", t=PACK))
         nc.scalar.dma_start(step1[:], sa.rearrange("(p t) o -> p (t o)", t=PACK))
-        order = [(name, t) for t in range(3) for name in "daeb"] + [(name, 3) for name in "deab"]
+        ident = keep.tile([P, P], F32, name="ident")
+        make_identity(nc, ident[:])
+        minus_step1 = keep.tile([P, PACK], F32, name="minus_step1", tag="minus_step1_then_pairs")
+        nc.scalar.activation(minus_step1[:], step1[:], COPY, scale=-1.0)
+
+        order = [(name, t) for t in range(EARLY) for name in "daeb"]
+        order = order + [("d", 2), ("a", 2), ("e", 2), ("d", 3), ("e", 3), ("a", 3), ("b", 2), ("b", 3)]
         rows = {}
         for name, t in order:
             rows[name, t] = keep.tile([P, V], U8, name="%s_rows%d" % (name, t))
@@ -55,137 +62,153 @@ def tile_list_turnedpairs_kernel(tc, ca, cb, cd, ce, sa, sb, w_words, w_scales, 
                 nc.sync.dma_start(list2[:], offs2)
             if (name, t) == ("a", 0):
                 nc.sync.dma_start(list1[:], offs)
-        nc.sync.dma_start(w1c[:].bitcast(I32), w_words[0].bitcast(I32))
-        nc.sync.dma_start(w2c[:].bitcast(I32), w2_words[0].rearrange("p n t -> p (n t)").bitcast(I32))
-        for q in range(4):
-            nc.sync.dma_start(w1s[32 * q : 32 * q + 4, :].bitcast(I32), w_scales[0, 4 * q : 4 * q + 4, :].bitcast(I32))
-        for q in range(4):
-            nc.sync.dma_start(w2s[32 * q : 32 * q + 4, :].bitcast(I32), w2_scales[0, 4 * q : 4 * q + 4, :].bitcast(I32))
+        nc.sync.dma_start(w1_codes[:].bitcast(I32), w_words[0].bitcast(I32))
+        nc.sync.dma_start(w2_codes[:].bitcast(I32), w2_words[0].rearrange("p n t -> p (n t)").bitcast(I32))
+        for scale_tile, source in ((w1_scale_rows, w_scales), (w2_scale_rows, w2_scales)):
+            for q in range(4):
+                nc.sync.dma_start(scale_tile[32 * q : 32 * q + 4, :].bitcast(I32), source[0, 4 * q : 4 * q + 4, :].bitcast(I32))
 
         times_a = keep.tile([P, PACK, 2, J], F32, name="times_a")
         times_b = keep.tile([P, 2, PACK, J], F32, name="times_b")
         products = {"a": times_a[:].rearrange("p t z j -> p z t j"), "b": times_b[:]}
         factors = {(name, t): keep.tile([P, 2, J], F32, name="for_%s%d" % (name, t))[:]
-                   for name in "ab" for t in range(PACK) if name == "a" or t < 2}
-        late_factors = keep.tile([P, 2, J], F32, name="late_factors")
-        late_b = keep.tile([P, 2 * J], U8, name="b_picked_late")
+                   for name in "ab" for t in range(PACK) if name == "a" or t < EARLY}
+        late_b = keep.tile([P, 2 * J], U8, name="late_b")
+        late_b_factors = [keep.tile([P, 2, J], F32, name="late_b_factors0")[:], times_a[:, 3]]
         codes, wide = {}, {}
 
         def factor_of(name, t, part):
-            if name == "b" and t >= 2:
-                return late_factors[:, t - 2, :] if part == 0 else times_a[:, 3, t - 2, :]
+            if name == "b" and t >= EARLY:
+                return late_b_factors[part][:, t - EARLY, :]
             return factors[name, t][:, part, :]
 
         def gather(name, t):
-            if name == "b" and t >= 2:
-                picked = late_b[:, (t - 2) * J : (t - 1) * J]
+            if name == "b" and t >= EARLY:
+                picked = late_b[:, (t - EARLY) * J : (t - EARLY + 1) * J]
             else:
                 picked = keep.tile([P, J], U8, name="%s_picked%d" % (name, t))[:]
             nc.vector.tensor_copy(picked, rows[name, t][:].indirect((list1 if name in "ab" else list2)[:]))
             codes[name, t] = picked.bitcast(FP8)
 
-        def factor(name, t, part):
+        def make_factor(name, t, part):
             source = "de"[part] if name == "a" else "ed"[part]
-            step = (step1, step2)[part]
+            step = step2 if part else (step1 if name == "a" else minus_step1)
             nc.scalar.activation(factor_of(name, t, part), codes[source, t], COPY, scale=step[:, t : t + 1])
 
         def widen(name, t):
             wide[name, t] = keep.tile([P, J], F32, name="%s_wide%d" % (name, t))
             nc.scalar.copy(wide[name, t][:], codes[name, t])
 
-        def on_gpsimd(name, t, part):
+        def one_part_on_gpsimd(name, t, part):
             nc.gpsimd.tensor_tensor(products[name][:, part, t, :], wide[name, t][:], factor_of(name, t, part), MULT)
 
-        def both_on_gpsimd(name, t):
+        def both_parts_on_gpsimd(name, t):
             spread = wide[name, t][:].unsqueeze(1).to_broadcast([P, 2, J])
             nc.gpsimd.tensor_tensor(products[name][:, :, t, :], spread, factors[name, t], MULT)
 
-        for t in range(3):
+        sums = [psum.tile([P, 2, EARLY, P], F32, name="sums%d" % h) for h in range(2)]
+
+        def turn_and_add(name, t):
+            for h in range(2):
+                for part in range(2):
+                    nc.tensor.matmul(sums[h][:, part, t, :], lhsT=products[name][:, part, t, h * HALF : (h + 1) * HALF],
+                                     rhs=ident[:], is_transpose=True, start=(name, t, part) == ("a", 0, 0),
+                                     stop=(name, t, part) == ("b", EARLY - 1, 1))
+
+        for t in range(EARLY + 1):
             gather("d", t)
-            factor("a", t, 0)
+            make_factor("a", t, 0)
             gather("a", t)
             widen("a", t)
             if t == 0:
-                on_gpsimd("a", t, 0)
+                one_part_on_gpsimd("a", t, 0)
             gather("e", t)
-            factor("a", t, 1)
+            make_factor("a", t, 1)
             if t == 0:
-                on_gpsimd("a", t, 1)
+                one_part_on_gpsimd("a", t, 1)
             else:
-                both_on_gpsimd("a", t)
-            if t < 2:
-                factor("b", t, 0)
-                factor("b", t, 1)
+                both_parts_on_gpsimd("a", t)
+            if t < EARLY:
+                make_factor("b", t, 0)
+                make_factor("b", t, 1)
                 gather("b", t)
                 widen("b", t)
-                both_on_gpsimd("b", t)
-        factor("b", 2, 0)
-        gather("b", 2)
-        widen("b", 2)
-        on_gpsimd("b", 2, 0)
+                both_parts_on_gpsimd("b", t)
+                turn_and_add("a", t)
+                turn_and_add("b", t)
         gather("d", 3)
         gather("e", 3)
-        factor("b", 2, 1)
-        factor("b", 3, 1)
-        factor("b", 3, 0)
-        factor("a", 3, 0)
-        factor("a", 3, 1)
+        make_factor("b", 2, 1)
+        make_factor("b", 3, 1)
+        make_factor("a", 3, 0)
+        make_factor("a", 3, 1)
+        make_factor("b", 2, 0)
+        make_factor("b", 3, 0)
         gather("a", 3)
+        gather("b", 2)
         gather("b", 3)
-        nc.vector.tensor_tensor(products["b"][:, 1, 2:4, :].rearrange("p t j -> p (t j)"), late_b[:].bitcast(FP8), times_a[:, 3].rearrange("p z j -> p (z j)"), MULT)
-        nc.vector.tensor_tensor(products["b"][:, 0, 3, :], codes["b", 3], factor_of("b", 3, 0), MULT)
+        for part in (1, 0):
+            nc.vector.tensor_tensor(products["b"][:, part, EARLY:PACK, :].rearrange("p t j -> p (t j)"), late_b[:].bitcast(FP8),
+                                    late_b_factors[part].rearrange("p t j -> p (t j)"), MULT)
         for part in range(2):
             nc.vector.tensor_tensor(products["a"][:, part, 3, :], codes["a", 3], factors["a", 3][:, part, :], MULT)
 
-        def woven(name, part, h):
-            return products[name][:, part, :, h * HALF : (h + 1) * HALF].rearrange("p t (c i) -> p c t i", i=2)
-
-        z, zc, zs = {}, {}, {}
+        z, z_codes, z_scales = {}, {}, {}
         for h in range(2):
             for part in range(2):
                 z[part, h] = keep.tile([P, HALF * PACK], BF16, name="z%d_%d" % (part, h), align_bytes=64)
-                zc[part, h] = keep.tile([P, HALF], U32, name="zc%d_%d" % (part, h), align_bytes=64)
-                zs[part, h] = keep.tile([P, HALF], U8, name="zs%d_%d" % (part, h), align_bytes=64)
+                z_codes[part, h] = keep.tile([P, HALF], U32, name="z_codes%d_%d" % (part, h), align_bytes=64)
+                z_scales[part, h] = keep.tile([P, HALF], U8, name="z_scales%d_%d" % (part, h), align_bytes=64)
 
-        def combine(part, h):
-            dst = z[part, h][:].rearrange("p (c i t) -> p c t i", t=PACK, i=2)
-            nc.vector.tensor_tensor(dst, woven("a", part, h), woven("b", part, h), ADD if part else SUB)
+        turned = [psum.tile([P, 2, HALF], F32, name="turned%d" % h) for h in range(2)]
+        pairs = keep.tile([P, 2, 2, P, EARLY], BF16, name="pairs", tag="minus_step1_then_pairs")
+        for h in range(2):
+            nc.scalar.copy(pairs[:, h], sums[h][:].rearrange("j z t p -> j z p t"))
+            pair_words = pairs[:, h].rearrange("j z p t -> j (z p t)").bitcast(F32)
+            for part in range(2):
+                nc.tensor.transpose(turned[h][:, part, :], pair_words[:, part * P : (part + 1) * P], ident[:])
+        paired = {}
+        for h in range(2):
+            for part in range(2):
+                paired[part, h] = keep.tile([P, 2, HALF, 2], BF16, name="paired%d_%d" % (part, h))
+                nc.scalar.copy(paired[part, h][:, 0].rearrange("p j e -> p (j e)").bitcast(F32), turned[h][:, part, :])
 
-        def quantise(part, h):
-            nc.vector.quantize_mx(zc[part, h][:].bitcast(E4M3X4), zs[part, h][:], z[part, h][:])
+        def add_late_planes(part, h):
+            terms = [products[name][:, part, EARLY:PACK, h * HALF : (h + 1) * HALF].rearrange("p e (c i) -> p c e i", i=2)
+                     for name in "ab"]
+            nc.vector.tensor_tensor(paired[part, h][:, 1].rearrange("p (c i) e -> p c e i", i=2), terms[0], terms[1], ADD)
+
+        def merge(copy, part, h):
+            src = paired[part, h][:].rearrange("p u j e -> p (u j e)").bitcast(F32).rearrange("p (u c i) -> p c u i", u=2, i=2)
+            copy(z[part, h][:].bitcast(F32).rearrange("p (c i u) -> p c u i", u=2, i=2), src)
 
         acc = {(h, m): psum.tile([P, HALF], F32, name="acc%d_%d" % (h, m)) for h in range(2) for m in range(2)}
 
-        def multiply(part, h):
+        def quantise_and_multiply(part, h):
+            nc.vector.quantize_mx(z_codes[part, h][:].bitcast(E4M3X4), z_scales[part, h][:], z[part, h][:])
             for m in range(2):
                 cols = slice(m * P, (m + 1) * P)
                 if part == 0:
-                    weights, scales = w1c[:, 2 * m * P : 2 * (m + 1) * P].bitcast(E2M1X4), w1s[:, cols]
+                    weights, scales = w1_codes[:, 2 * m * P : 2 * (m + 1) * P].bitcast(E2M1X4), w1_scale_rows[:, cols]
                 else:
-                    weights, scales = w2c[:, cols].bitcast(E5M2X4), w2s[:, cols]
-                nc.tensor.matmul_mx(acc[h, m][:], lhsT=weights, lhsT_scale=scales, rhs=zc[part, h][:].bitcast(E4M3X4),
-                                    rhs_scale=zs[part, h][:], start=part == 0, stop=part == 1)
+                    weights, scales = w2_codes[:, cols].bitcast(E5M2X4), w2_scale_rows[:, cols]
+                nc.tensor.matmul_mx(acc[h, m][:], lhsT=weights, lhsT_scale=scales, rhs=z_codes[part, h][:].bitcast(E4M3X4),
+                                    rhs_scale=z_scales[part, h][:], start=part == 0, stop=part == 1)
 
         def store(h):
-            res = keep.tile([P, 2, HALF], F32, name="res%d" % h)
-            nc.scalar.copy(res[:, 0, :], acc[h, 0][:])
+            result = keep.tile([P, 2, HALF], F32, name="result%d" % h)
+            nc.scalar.copy(result[:, 0, :], acc[h, 0][:])
             if h == 0:
-                nc.scalar.copy(res[:, 1, :], acc[h, 1][:])
+                nc.scalar.copy(result[:, 1, :], acc[h, 1][:])
             else:
-                nc.vector.tensor_copy(res[:, 1, :], acc[h, 1][:])
-            nc.sync.dma_start(out.rearrange("(m p) j -> p m j", p=P)[:, :, h * HALF : (h + 1) * HALF], res[:])
+                nc.vector.tensor_copy(result[:, 1, :], acc[h, 1][:])
+            nc.sync.dma_start(out.rearrange("(m p) j -> p m j", p=P)[:, :, h * HALF : (h + 1) * HALF], result[:])
 
-        combine(0, 0)
-        combine(1, 0)
-        quantise(0, 0)
-        multiply(0, 0)
-        combine(0, 1)
-        quantise(1, 0)
-        multiply(1, 0)
-        store(0)
-        combine(1, 1)
-        quantise(0, 1)
-        multiply(0, 1)
-        quantise(1, 1)
-        multiply(1, 1)
-        store(1)
+        for h in range(2):
+            for part in range(2):
+                add_late_planes(part, h)
+                merge(nc.vector.tensor_copy if (part, h) == (1, 1) else nc.scalar.copy, part, h)
+        for h in range(2):
+            for part in range(2):
+                quantise_and_multiply(part, h)
+            store(h)

from contextlib import ExitStack

import concourse.mybir as mybir
from concourse.masks import make_identity

K, V, J, N = 512, 512, 256, 256
FLOPS = 2 * 2 * K * N * J

F32 = mybir.dt.float32
BF16 = mybir.dt.bfloat16
I32 = mybir.dt.int32
U32 = mybir.dt.uint32
U16 = mybir.dt.uint16
U8 = mybir.dt.uint8
FP8 = mybir.dt.float8_e4m3fn
E4M3X4 = mybir.dt.float8_e4m3fn_x4
E5M2X4 = mybir.dt.float8_e5m2_x4
E2M1X4 = mybir.dt.float4_e2m1fn_x4
MULT = mybir.AluOpType.mult
ADD = mybir.AluOpType.add
COPY = mybir.ActivationFunctionType.Copy

P = 128
PACK = 4
HALF = J // 2
EARLY = 2


def tile_list_turnedpairs_kernel(tc, ca, cb, cd, ce, sa, sb, w_words, w_scales, w2_words, w2_scales, offs, offs2, out):
    nc = tc.nc
    tables = {"a": ca, "b": cb, "d": cd, "e": ce}
    with ExitStack() as ctx:
        keep = ctx.enter_context(tc.tile_pool(name="keep", bufs=1))
        psum = ctx.enter_context(tc.psum_pool(name="psum", bufs=1))

        list1 = keep.tile([P, J // 16], U16, name="list1")
        list2 = keep.tile([P, J // 16], U16, name="list2")
        step1 = keep.tile([P, PACK], F32, name="step1")
        step2 = keep.tile([P, PACK], F32, name="step2")
        w1_scale_rows = keep.tile([P, N], U8, name="w1_scale_rows", align_bytes=64)
        w2_scale_rows = keep.tile([P, N], U8, name="w2_scale_rows", align_bytes=64)
        w1_codes = keep.tile([P, 2 * N], U8, name="w1_codes", align_bytes=64)
        w2_codes = keep.tile([P, N], U32, name="w2_codes", align_bytes=64)

        nc.vector.memset(w1_scale_rows[:].bitcast(I32), 0)
        nc.vector.memset(w2_scale_rows[:].bitcast(I32), 0)

        nc.gpsimd.dma_start(step2[:], sb.rearrange("(p t) o -> p (t o)", t=PACK))
        nc.scalar.dma_start(step1[:], sa.rearrange("(p t) o -> p (t o)", t=PACK))
        ident = keep.tile([P, P], F32, name="ident")
        make_identity(nc, ident[:])
        minus_step1 = keep.tile([P, PACK], F32, name="minus_step1", tag="minus_step1_then_pairs")
        nc.scalar.activation(minus_step1[:], step1[:], COPY, scale=-1.0)

        order = [(name, t) for t in range(EARLY) for name in "daeb"]
        order = order + [("d", 2), ("a", 2), ("e", 2), ("d", 3), ("e", 3), ("a", 3), ("b", 2), ("b", 3)]
        rows = {}
        for name, t in order:
            rows[name, t] = keep.tile([P, V], U8, name="%s_rows%d" % (name, t))
            nc.sync.dma_start(rows[name, t][:], tables[name].rearrange("(p t) v -> t p v", t=PACK)[t])
            if (name, t) == ("d", 0):
                nc.sync.dma_start(list2[:], offs2)
            if (name, t) == ("a", 0):
                nc.sync.dma_start(list1[:], offs)
        nc.sync.dma_start(w1_codes[:].bitcast(I32), w_words[0].bitcast(I32))
        nc.sync.dma_start(w2_codes[:].bitcast(I32), w2_words[0].rearrange("p n t -> p (n t)").bitcast(I32))
        for scale_tile, source in ((w1_scale_rows, w_scales), (w2_scale_rows, w2_scales)):
            for q in range(4):
                nc.sync.dma_start(scale_tile[32 * q : 32 * q + 4, :].bitcast(I32), source[0, 4 * q : 4 * q + 4, :].bitcast(I32))

        times_a = keep.tile([P, PACK, 2, J], F32, name="times_a")
        times_b = keep.tile([P, 2, PACK, J], F32, name="times_b")
        products = {"a": times_a[:].rearrange("p t z j -> p z t j"), "b": times_b[:]}
        factors = {(name, t): keep.tile([P, 2, J], F32, name="for_%s%d" % (name, t))[:]
                   for name in "ab" for t in range(PACK) if name == "a" or t < EARLY}
        late_b = keep.tile([P, 2 * J], U8, name="late_b")
        late_b_factors = [keep.tile([P, 2, J], F32, name="late_b_factors0")[:], times_a[:, 3]]
        codes, wide = {}, {}

        def factor_of(name, t, part):
            if name == "b" and t >= EARLY:
                return late_b_factors[part][:, t - EARLY, :]
            return factors[name, t][:, part, :]

        def gather(name, t):
            if name == "b" and t >= EARLY:
                picked = late_b[:, (t - EARLY) * J : (t - EARLY + 1) * J]
            else:
                picked = keep.tile([P, J], U8, name="%s_picked%d" % (name, t))[:]
            nc.vector.tensor_copy(picked, rows[name, t][:].indirect((list1 if name in "ab" else list2)[:]))
            codes[name, t] = picked.bitcast(FP8)

        def make_factor(name, t, part):
            source = "de"[part] if name == "a" else "ed"[part]
            step = step2 if part else (step1 if name == "a" else minus_step1)
            nc.scalar.activation(factor_of(name, t, part), codes[source, t], COPY, scale=step[:, t : t + 1])

        def widen(name, t):
            wide[name, t] = keep.tile([P, J], F32, name="%s_wide%d" % (name, t))
            nc.scalar.copy(wide[name, t][:], codes[name, t])

        def one_part_on_gpsimd(name, t, part):
            nc.gpsimd.tensor_tensor(products[name][:, part, t, :], wide[name, t][:], factor_of(name, t, part), MULT)

        def both_parts_on_gpsimd(name, t):
            spread = wide[name, t][:].unsqueeze(1).to_broadcast([P, 2, J])
            nc.gpsimd.tensor_tensor(products[name][:, :, t, :], spread, factors[name, t], MULT)

        sums = [psum.tile([P, 2, EARLY, P], F32, name="sums%d" % h) for h in range(2)]

        def turn_and_add(name, t):
            for h in range(2):
                for part in range(2):
                    nc.tensor.matmul(sums[h][:, part, t, :], lhsT=products[name][:, part, t, h * HALF : (h + 1) * HALF],
                                     rhs=ident[:], is_transpose=True, start=(name, t, part) == ("a", 0, 0),
                                     stop=(name, t, part) == ("b", EARLY - 1, 1))

        for t in range(EARLY + 1):
            gather("d", t)
            make_factor("a", t, 0)
            gather("a", t)
            widen("a", t)
            if t == 0:
                one_part_on_gpsimd("a", t, 0)
            gather("e", t)
            make_factor("a", t, 1)
            if t == 0:
                one_part_on_gpsimd("a", t, 1)
            else:
                both_parts_on_gpsimd("a", t)
            if t < EARLY:
                make_factor("b", t, 0)
                make_factor("b", t, 1)
                gather("b", t)
                widen("b", t)
                both_parts_on_gpsimd("b", t)
                turn_and_add("a", t)
                turn_and_add("b", t)
        gather("d", 3)
        gather("e", 3)
        make_factor("b", 2, 1)
        make_factor("b", 3, 1)
        make_factor("a", 3, 0)
        make_factor("a", 3, 1)
        make_factor("b", 2, 0)
        make_factor("b", 3, 0)
        gather("a", 3)
        gather("b", 2)
        gather("b", 3)
        for part in (1, 0):
            nc.vector.tensor_tensor(products["b"][:, part, EARLY:PACK, :].rearrange("p t j -> p (t j)"), late_b[:].bitcast(FP8),
                                    late_b_factors[part].rearrange("p t j -> p (t j)"), MULT)
        for part in range(2):
            nc.vector.tensor_tensor(products["a"][:, part, 3, :], codes["a", 3], factors["a", 3][:, part, :], MULT)

        z, z_codes, z_scales = {}, {}, {}
        for h in range(2):
            for part in range(2):
                z[part, h] = keep.tile([P, HALF * PACK], BF16, name="z%d_%d" % (part, h), align_bytes=64)
                z_codes[part, h] = keep.tile([P, HALF], U32, name="z_codes%d_%d" % (part, h), align_bytes=64)
                z_scales[part, h] = keep.tile([P, HALF], U8, name="z_scales%d_%d" % (part, h), align_bytes=64)

        turned = [psum.tile([P, 2, HALF], F32, name="turned%d" % h) for h in range(2)]
        pairs = keep.tile([P, 2, 2, P, EARLY], BF16, name="pairs", tag="minus_step1_then_pairs")
        for h in range(2):
            nc.scalar.copy(pairs[:, h], sums[h][:].rearrange("j z t p -> j z p t"))
            pair_words = pairs[:, h].rearrange("j z p t -> j (z p t)").bitcast(F32)
            for part in range(2):
                nc.tensor.transpose(turned[h][:, part, :], pair_words[:, part * P : (part + 1) * P], ident[:])
        paired = {}
        for h in range(2):
            for part in range(2):
                paired[part, h] = keep.tile([P, 2, HALF, 2], BF16, name="paired%d_%d" % (part, h))
                nc.scalar.copy(paired[part, h][:, 0].rearrange("p j e -> p (j e)").bitcast(F32), turned[h][:, part, :])

        def add_late_planes(part, h):
            terms = [products[name][:, part, EARLY:PACK, h * HALF : (h + 1) * HALF].rearrange("p e (c i) -> p c e i", i=2)
                     for name in "ab"]
            nc.vector.tensor_tensor(paired[part, h][:, 1].rearrange("p (c i) e -> p c e i", i=2), terms[0], terms[1], ADD)

        def merge(copy, part, h):
            src = paired[part, h][:].rearrange("p u j e -> p (u j e)").bitcast(F32).rearrange("p (u c i) -> p c u i", u=2, i=2)
            copy(z[part, h][:].bitcast(F32).rearrange("p (c i u) -> p c u i", u=2, i=2), src)

        acc = {(h, m): psum.tile([P, HALF], F32, name="acc%d_%d" % (h, m)) for h in range(2) for m in range(2)}

        def quantise_and_multiply(part, h):
            nc.vector.quantize_mx(z_codes[part, h][:].bitcast(E4M3X4), z_scales[part, h][:], z[part, h][:])
            for m in range(2):
                cols = slice(m * P, (m + 1) * P)
                if part == 0:
                    weights, scales = w1_codes[:, 2 * m * P : 2 * (m + 1) * P].bitcast(E2M1X4), w1_scale_rows[:, cols]
                else:
                    weights, scales = w2_codes[:, cols].bitcast(E5M2X4), w2_scale_rows[:, cols]
                nc.tensor.matmul_mx(acc[h, m][:], lhsT=weights, lhsT_scale=scales, rhs=z_codes[part, h][:].bitcast(E4M3X4),
                                    rhs_scale=z_scales[part, h][:], start=part == 0, stop=part == 1)

        def store(h):
            result = keep.tile([P, 2, HALF], F32, name="result%d" % h)
            nc.scalar.copy(result[:, 0, :], acc[h, 0][:])
            if h == 0:
                nc.scalar.copy(result[:, 1, :], acc[h, 1][:])
            else:
                nc.vector.tensor_copy(result[:, 1, :], acc[h, 1][:])
            nc.sync.dma_start(out.rearrange("(m p) j -> p m j", p=P)[:, :, h * HALF : (h + 1) * HALF], result[:])

        for h in range(2):
            for part in range(2):
                add_late_planes(part, h)
                merge(nc.vector.tensor_copy if (part, h) == (1, 1) else nc.scalar.copy, part, h)
        for h in range(2):
            for part in range(2):
                quantise_and_multiply(part, h)
            store(h)
